import numpy as np
import ml_dtypes


def mxq(x, axis, fmt="e4m3"):
    dtype, down = {"e4m3": (ml_dtypes.float8_e4m3fn, 7), "e5m2": (ml_dtypes.float8_e5m2, 14)}[fmt]
    v = np.moveaxis(np.asarray(x, np.float32).astype(ml_dtypes.bfloat16).astype(np.float64), axis, -1)
    blocks = v.reshape(v.shape[:-1] + (-1, 32))
    amax = np.abs(blocks).max(-1, keepdims=True)
    byte = np.maximum(np.where(amax > 0, np.frexp(amax)[1] - 1 + 127, 0) - down, 1)
    scale = np.exp2(byte - 127.0)
    codes = (blocks / scale).astype(np.float32).astype(dtype).astype(np.float64)
    return np.moveaxis((codes * scale).reshape(v.shape), -1, axis)


WIDE = False


def mx_kscale(k):
    if not WIDE:
        return np.ones(k)
    levels = np.array([10, -10, 5, -5, 0])
    if k % 512:
        return np.exp2(np.random.permutation(np.resize(levels, k // 32))).repeat(32)
    a = np.empty((k // 512, 16))
    for p in range(k // 512):
        a[p, :8] = np.random.permutation(np.resize(levels, 8))
        for g in range(8):
            far = levels[np.abs(levels - a[p, g]) >= 10]
            a[p, g + 8] = far[np.random.randint(len(far))]
    return np.exp2(a.ravel()).repeat(32)


def f64(x):
    return np.asarray(x).astype(np.float64)


def striped8(idx):
    return np.asarray(idx).reshape(8, -1, 16).transpose(0, 2, 1).reshape(128, -1).astype(np.uint16)


def unstriped8(offs):
    return offs.reshape(8, 16, -1).transpose(0, 2, 1).reshape(8, -1).astype(np.int64)


def pick8(x, idx, run):
    r = np.arange(len(x))
    return x[r[:, None], idx[r % (8 * run) // run]]


E2M1 = np.array([0.0, 0.5, 1.0, 1.5, 2.0, 3.0, 4.0, 6.0, -0.0, -0.5, -1.0, -1.5, -2.0, -3.0, -4.0, -6.0])


def pack_weight(w, fmt):
    k, n = w.shape
    w = f64(np.asarray(w, np.float32).astype(ml_dtypes.bfloat16)).reshape(k // 32, 32, n)
    amax = np.abs(w).max(1)
    if fmt == "e4m3":
        byte = np.frexp(amax)[1] - 1 + 127 - 7
    else:
        mant, ex = np.frexp(amax / 6.0)
        byte = np.where(mant > 0.5, ex, ex - 1) + 127
    byte = np.clip(np.where(amax > 0, byte, 1), 1, 254)
    scaled = (w * np.exp2(127.0 - byte)[:, None, :]).reshape(k, n).astype(np.float32)
    by_word = np.ascontiguousarray(scaled.reshape(k // 512, 128, 4, n).transpose(0, 1, 3, 2))
    if fmt == "e4m3":
        words = by_word.astype(ml_dtypes.float8_e4m3fn).view(np.uint8)
    else:
        c = by_word.astype(ml_dtypes.float4_e2m1fn).view(np.uint8) & 0xF
        words = (c[..., 0::2] | (c[..., 1::2] << 4)).reshape(k // 512, 128, 2 * n)
    return np.ascontiguousarray(words), np.ascontiguousarray(byte.astype(np.uint8).reshape(k // 512, 16, n))


def unpack_weight(words, scales, fmt):
    g, _, n = scales.shape
    words = np.ascontiguousarray(words).reshape(g, 128, n, -1)
    if fmt == "e4m3":
        vals = words.view(ml_dtypes.float8_e4m3fn).astype(np.float64)
    else:
        nib = np.empty((g, 128, n, 4), np.uint8)
        nib[..., 0::2] = words & 0xF
        nib[..., 1::2] = words >> 4
        vals = E2M1[nib]
    vals = vals * np.repeat(np.exp2(scales.astype(np.float64) - 127.0), 8, axis=1)[..., None]
    return vals.transpose(0, 1, 3, 2).reshape(g * 512, n)


K, T, J, B, L, N = 512, 512, 512, 128, 512, 512


def setup_inputs():
    n = np.random.standard_normal
    idx = np.stack([np.random.randint(0, T, J) for _ in range(8)])
    fk = mx_kscale(K)
    fl = mx_kscale(L)
    xtp = pack_weight(n((K, T)) / fk[:, None], "e4m3")
    wp = pack_weight(n((K, N)) * 1 / np.sqrt(K) * fk[:, None], "e2m1")
    wsp = pack_weight(n((L, N)) * 1 / np.sqrt(L) * fl[:, None], "e4m3")
    return {
        "xt_words": xtp[0],
        "xt_scales": xtp[1],
        "w_words": wp[0],
        "w_scales": wp[1],
        "sx": (n((L, J)) / fl[:, None]).astype(np.float32),
        "ws_words": wsp[0],
        "ws_scales": wsp[1],
        "offs": striped8(idx),
    }


def reference(xt_words, xt_scales, w_words, w_scales, sx, ws_words, ws_scales, offs):
    idx = unstriped8(offs)
    xtu = unpack_weight(xt_words, xt_scales, "e4m3")
    wu = unpack_weight(w_words, w_scales, "e2m1")
    wsu = unpack_weight(ws_words, ws_scales, "e4m3")
    z = wu.T @ xtu
    u = pick8(z, idx, 64)
    m = u.reshape(N, B, J // B).mean(axis=2)
    mr = np.repeat(m, J // B, axis=1)
    sxq = mxq(f64(sx), 0, "e4m3")
    q = wsu.T @ sxq
    y = np.tanh(u - mr) + 0.5 * q
    return y

@@ -1,0 +1,189 @@
+from contextlib import ExitStack
+
+import concourse.mybir as mybir
+from concourse.masks import make_identity
+
+K, T, J, L, N = 512, 512, 512, 512, 512
+FLOPS = 2 * K * N * T + 2 * L * N * J
+
+F32 = mybir.dt.float32
+BF16 = mybir.dt.bfloat16
+I32 = mybir.dt.int32
+U32 = mybir.dt.uint32
+U16 = mybir.dt.uint16
+U8 = mybir.dt.uint8
+FP8X4 = mybir.dt.float8_e4m3fn_x4
+FP4X4 = mybir.dt.float4_e2m1fn_x4
+ALU = mybir.AluOpType
+ACT = mybir.ActivationFunctionType
+
+P = 128
+TILES = 4
+RUNS = 16
+GROUP = 4
+
+
+def load_scale_rows(engines, plane, scales):
+    rows = scales[0].bitcast(I32)
+    for quad in range(4):
+        engines[quad].dma_start(out=plane[32 * quad : 32 * quad + 4, :].bitcast(I32), in_=rows[4 * quad : 4 * quad + 4, :])
+
+
+def deal(nc, dst, src):
+    nc.vector.tensor_copy(
+        out=dst[:].bitcast(I32).rearrange("p (s a c) -> p s a c", s=TILES, a=RUNS),
+        in_=src[:].bitcast(I32).rearrange("p (a s c) -> p s a c", s=TILES, a=RUNS),
+    )
+
+
+def tile_list_head_members_and_group_kernel(tc, xt_words, xt_scales, w_words, w_scales, sx, ws_words, ws_scales, offs, out):
+    nc = tc.nc
+    with ExitStack() as ctx:
+        keep = ctx.enter_context(tc.tile_pool(name="keep", bufs=1))
+        psum = ctx.enter_context(tc.psum_pool(name="psum", bufs=1))
+
+        offsets = keep.tile([P, J // 16], U16, name="offsets")
+        xt_codes = keep.tile([P, T], U32, name="xt_codes", align_bytes=64)
+        xt_plane = keep.tile([P, T], U8, name="xt_plane", align_bytes=64)
+        w_raw = keep.tile([P, 2 * N], U8, name="w_raw", align_bytes=64)
+        w_plane_raw = keep.tile([P, N], U8, name="w_plane_raw", align_bytes=64)
+        w_codes = keep.tile([P, 2 * N], U8, name="w_codes", align_bytes=64)
+        w_plane = keep.tile([P, N], U8, name="w_plane", align_bytes=64)
+        ws_plane_raw = keep.tile([P, N], U8, name="ws_plane_raw", align_bytes=64)
+        ws_codes = keep.tile([P, N], U32, name="ws_codes", align_bytes=64)
+        ws_plane = keep.tile([P, N], U8, name="ws_plane", align_bytes=64)
+        sx_bf = keep.tile([P, J, 4], BF16, name="sx_bf", align_bytes=64)
+        sx_codes = keep.tile([P, J], U32, name="sx_codes", align_bytes=64)
+        sx_plane = keep.tile([P, J], U8, name="sx_plane", align_bytes=64)
+
+        ident = keep.tile([P, P], F32, name="ident")
+        warm_in = keep.tile([P, 8], F32, name="warm_in", tag="ws_raw", align_bytes=64)
+        warm_out = keep.tile([P, 8], F32, name="warm_out", tag="sx_raw", align_bytes=64)
+        nc.gpsimd.memset(w_plane_raw[:].bitcast(I32), 0)
+        nc.gpsimd.memset(xt_plane[:].bitcast(I32), 0)
+        nc.gpsimd.memset(warm_in[:], 0.0)
+        nc.gpsimd.memset(ws_plane_raw[:].bitcast(I32), 0)
+
+        nc.sync.dma_start(out=w_raw[:].bitcast(I32), in_=w_words[0].bitcast(I32))
+        nc.scalar.dma_start(out=xt_codes[:].bitcast(I32), in_=xt_words[0].rearrange("p c r -> p (c r)").bitcast(I32))
+        load_scale_rows([nc.sync] * 4, w_plane_raw, w_scales)
+        load_scale_rows([nc.sync] * 4, xt_plane, xt_scales)
+        nc.scalar.activation(out=warm_out[:], in_=warm_in[:], func=ACT.Tanh)
+        nc.sync.dma_start(offsets[:], offs)
+        ws_raw = keep.tile([P, N], U32, name="ws_raw", tag="ws_raw", align_bytes=64)
+        sx_raw = keep.tile([P, 4, J], F32, name="sx_raw", tag="sx_raw", align_bytes=64)
+        nc.sync.dma_start(out=ws_raw[:].bitcast(I32), in_=ws_words[0].rearrange("p c r -> p (c r)").bitcast(I32))
+        nc.sync.dma_start(out=sx_raw[:], in_=sx.rearrange("(p i) j -> p i j", i=4))
+        load_scale_rows([nc.gpsimd] * 4, ws_plane_raw, ws_scales)
+        make_identity(nc, ident[:])
+
+        deal(nc, w_codes, w_raw)
+        deal(nc, w_plane, w_plane_raw)
+
+        z_sb = []
+        for s in range(TILES):
+            z_ps = psum.tile([P, T], F32, name="z_ps%d" % s, tag="product%d" % s)
+            nc.tensor.matmul_mx(
+                out=z_ps[:],
+                lhsT=w_codes[:, 2 * P * s : 2 * P * (s + 1)].bitcast(FP4X4),
+                lhsT_scale=w_plane[:, P * s : P * (s + 1)],
+                rhs=xt_codes[:].bitcast(FP8X4),
+                rhs_scale=xt_plane[:],
+                start=True,
+                stop=True,
+            )
+            z = keep.tile([P, T], F32, name="z%d" % s)
+            nc.scalar.copy(out=z[:], in_=z_ps[:])
+            z_sb.append(z)
+
+        u, sums, d, th = [], [], [], []
+        for s in range(TILES):
+            u.append(keep.tile([P, J], F32, name="u%d" % s))
+            d.append(keep.tile([P, J], F32, name="d%d" % s))
+            th.append(keep.tile([P, J], F32, name="th%d" % s))
+
+        def gather(s):
+            for h in range(2):
+                nc.vector.tensor_copy(
+                    out=u[s][:, 256 * h : 256 * (h + 1)],
+                    in_=z_sb[s][:].indirect(offsets[:, 16 * h : 16 * (h + 1)]),
+                )
+
+        def group_sums(s):
+            nc.vector.tensor_reduce(
+                out=sums[s], in_=u[s][:].rearrange("p (b i) -> p b i", i=GROUP), axis=mybir.AxisListType.X, op=ALU.add
+            )
+
+        def centre(s):
+            nc.vector.scalar_tensor_tensor(
+                out=d[s][:].rearrange("p (b i) -> p b i", i=GROUP),
+                in0=sums[s].unsqueeze(2).to_broadcast([P, J // GROUP, GROUP]),
+                scalar=-1.0 / GROUP,
+                in1=u[s][:].rearrange("p (b i) -> p b i", i=GROUP),
+                op0=ALU.mult,
+                op1=ALU.add,
+            )
+            nc.scalar.activation(out=th[s][:], in_=d[s][:], func=ACT.Tanh)
+
+        banks = [psum.tile([P, 2, P], F32, name="mean_ps%d" % s) for s in range(TILES - 1)]
+
+        def sums_turned(s):
+            for i in range(GROUP):
+                nc.tensor.matmul(
+                    banks[s][:, 0, :], lhsT=u[s][:, i::GROUP], rhs=ident[:], is_transpose=True, start=(i == 0), stop=(i == GROUP - 1)
+                )
+
+        def means_turned(s):
+            nc.scalar.activation(out=sums[s], in_=banks[s][:, 0, :], func=ACT.Copy, scale=-1.0 / GROUP)
+
+        def means_back(s):
+            nc.tensor.transpose(banks[s][:, 1, :], sums[s], ident[:])
+
+        def centre_psum(s):
+            nc.vector.tensor_tensor(
+                out=d[s][:].rearrange("p (b i) -> p b i", i=GROUP),
+                in0=u[s][:].rearrange("p (b i) -> p b i", i=GROUP),
+                in1=banks[s][:, 1, :].unsqueeze(2).to_broadcast([P, J // GROUP, GROUP]),
+                op=ALU.add,
+            )
+            nc.scalar.activation(out=th[s][:], in_=d[s][:], func=ACT.Tanh)
+
+        deal(nc, ws_codes, ws_raw)
+        deal(nc, ws_plane, ws_plane_raw)
+        for s in range(TILES):
+            gather(s)
+        for s in range(TILES - 1):
+            sums_turned(s)
+        nc.scalar.copy(
+            out=sx_bf[:].rearrange("p (c i) t -> p c t i", i=4),
+            in_=sx_raw[:].rearrange("p t (c i) -> p c t i", i=4),
+        )
+        stats = keep.tile([P, TILES, P], F32, name="stats", tag="sx_raw", align_bytes=64)
+        sums.extend(stats[:, s, :] for s in range(TILES))
+        for s in range(TILES - 1):
+            means_turned(s)
+            means_back(s)
+        nc.vector.quantize_mx(
+            out=sx_codes[:].bitcast(FP8X4), scales=sx_plane[:], in_=sx_bf[:].rearrange("p j t -> p (j t)")
+        )
+        group_sums(3)
+        centre_psum(0)
+        centre(3)
+        centre_psum(1)
+        centre_psum(2)
+
+        out_rows = out.rearrange("(a s c) j -> s a c j", a=RUNS, s=TILES)
+        for s in (0, 3, 1, 2):
+            q_ps = psum.tile([P, J], F32, name="q_ps%d" % s, tag="product%d" % s)
+            nc.tensor.matmul_mx(
+                out=q_ps[:],
+                lhsT=ws_codes[:, P * s : P * (s + 1)].bitcast(FP8X4),
+                lhsT_scale=ws_plane[:, P * s : P * (s + 1)],
+                rhs=sx_codes[:].bitcast(FP8X4),
+                rhs_scale=sx_plane[:],
+                start=True,
+                stop=True,
+            )
+            y = keep.tile([P, J], F32, name="y%d" % s)
+            nc.vector.scalar_tensor_tensor(out=y[:], in0=q_ps[:], scalar=0.5, in1=th[s][:], op0=ALU.mult, op1=ALU.add)
+            nc.sync.dma_start(out=out_rows[s], in_=y[:])

@@ -31,8 +31,8 @@ def load_scale_rows(engines, plane, scales):
 
 def deal(nc, dst, src):
     nc.vector.tensor_copy(
-        out=dst[:].bitcast(I32).rearrange("p (s a c) -> p s a c", s=TILES, a=RUNS),
-        in_=src[:].bitcast(I32).rearrange("p (a s c) -> p s a c", s=TILES, a=RUNS),
+        out=dst.bitcast(I32).rearrange("p (s a c) -> p s a c", s=TILES, a=RUNS),
+        in_=src.bitcast(I32).rearrange("p (a s c) -> p s a c", s=TILES, a=RUNS),
     )
 
 
@@ -51,7 +51,6 @@ def tile_list_head_members_and_group_kernel(tc, xt_words, xt_scales, w_words, w_
         w_plane = keep.tile([P, N], U8, name="w_plane", align_bytes=64)
         ws_plane_raw = keep.tile([P, N], U8, name="ws_plane_raw", align_bytes=64)
         ws_codes = keep.tile([P, N], U32, name="ws_codes", align_bytes=64)
-        ws_plane = keep.tile([P, N], U8, name="ws_plane", align_bytes=64)
         sx_bf = keep.tile([P, J, 4], BF16, name="sx_bf", align_bytes=64)
         sx_codes = keep.tile([P, J], U32, name="sx_codes", align_bytes=64)
         sx_plane = keep.tile([P, J], U8, name="sx_plane", align_bytes=64)
@@ -59,14 +58,15 @@ def tile_list_head_members_and_group_kernel(tc, xt_words, xt_scales, w_words, w_
         ident = keep.tile([P, P], F32, name="ident")
         warm_in = keep.tile([P, 8], F32, name="warm_in", tag="ws_raw", align_bytes=64)
         warm_out = keep.tile([P, 8], F32, name="warm_out", tag="sx_raw", align_bytes=64)
-        nc.gpsimd.memset(w_plane_raw[:].bitcast(I32), 0)
         nc.gpsimd.memset(xt_plane[:].bitcast(I32), 0)
         nc.gpsimd.memset(warm_in[:], 0.0)
+        nc.vector.memset(w_plane[:].bitcast(I32), 0)
         nc.gpsimd.memset(ws_plane_raw[:].bitcast(I32), 0)
+        make_identity(nc, ident[:])
 
+        load_scale_rows([nc.sync] * 4, w_plane_raw, w_scales)
         nc.sync.dma_start(out=w_raw[:].bitcast(I32), in_=w_words[0].bitcast(I32))
         nc.scalar.dma_start(out=xt_codes[:].bitcast(I32), in_=xt_words[0].rearrange("p c r -> p (c r)").bitcast(I32))
-        load_scale_rows([nc.sync] * 4, w_plane_raw, w_scales)
         load_scale_rows([nc.sync] * 4, xt_plane, xt_scales)
         nc.scalar.activation(out=warm_out[:], in_=warm_in[:], func=ACT.Tanh)
         nc.sync.dma_start(offsets[:], offs)
@@ -74,27 +74,37 @@ def tile_list_head_members_and_group_kernel(tc, xt_words, xt_scales, w_words, w_
         sx_raw = keep.tile([P, 4, J], F32, name="sx_raw", tag="sx_raw", align_bytes=64)
         nc.sync.dma_start(out=ws_raw[:].bitcast(I32), in_=ws_words[0].rearrange("p c r -> p (c r)").bitcast(I32))
         nc.sync.dma_start(out=sx_raw[:], in_=sx.rearrange("(p i) j -> p i j", i=4))
-        load_scale_rows([nc.gpsimd] * 4, ws_plane_raw, ws_scales)
-        make_identity(nc, ident[:])
+        load_scale_rows([nc.sync] * 4, ws_plane_raw, ws_scales)
 
-        deal(nc, w_codes, w_raw)
-        deal(nc, w_plane, w_plane_raw)
+        for quad in range(4):
+            rows = slice(32 * quad, 32 * quad + 4)
+            deal(nc, w_plane[rows, :], w_plane_raw[rows, :])
+        deal(nc, w_codes[:], w_raw[:])
+        deal(nc, ws_codes[:], ws_raw[:])
 
-        z_sb = []
-        for s in range(TILES):
-            z_ps = psum.tile([P, T], F32, name="z_ps%d" % s, tag="product%d" % s)
+        def z_product(s, z_ps, cols):
             nc.tensor.matmul_mx(
-                out=z_ps[:],
+                out=z_ps,
                 lhsT=w_codes[:, 2 * P * s : 2 * P * (s + 1)].bitcast(FP4X4),
                 lhsT_scale=w_plane[:, P * s : P * (s + 1)],
-                rhs=xt_codes[:].bitcast(FP8X4),
-                rhs_scale=xt_plane[:],
+                rhs=xt_codes[:, cols].bitcast(FP8X4),
+                rhs_scale=xt_plane[:, cols],
                 start=True,
                 stop=True,
             )
-            z = keep.tile([P, T], F32, name="z%d" % s)
-            nc.scalar.copy(out=z[:], in_=z_ps[:])
-            z_sb.append(z)
+
+        z_sb = [keep.tile([P, T], F32, name="z%d" % s, tag="z%d" % s, align_bytes=64) for s in range(TILES)]
+        first_half = psum.tile([P, T // 2], F32, name="first_half", tag="spare")
+        z_product(0, first_half[:], slice(0, T // 2))
+        nc.scalar.copy(out=z_sb[0][:, : T // 2], in_=first_half[:])
+        for s in range(TILES):
+            z_ps = psum.tile([P, T], F32, name="z_ps%d" % s, tag="product%d" % s)
+            if s == 0:
+                z_product(s, z_ps[:, T // 2 :], slice(T // 2, T))
+                nc.vector.tensor_copy(out=z_sb[s][:, T // 2 :], in_=z_ps[:, T // 2 :])
+            else:
+                z_product(s, z_ps[:], slice(0, T))
+                nc.scalar.copy(out=z_sb[s][:], in_=z_ps[:])
 
         u, sums, d, th = [], [], [], []
         for s in range(TILES):
@@ -126,6 +136,9 @@ def tile_list_head_members_and_group_kernel(tc, xt_words, xt_scales, w_words, w_
             nc.scalar.activation(out=th[s][:], in_=d[s][:], func=ACT.Tanh)
 
         banks = [psum.tile([P, 2, P], F32, name="mean_ps%d" % s) for s in range(TILES - 1)]
+        banks.append(banks[0])
+        first_means = psum.tile([P, P], F32, name="first_means", tag="spare")
+        means = [first_means[:]] + [banks[s][:, 1, :] for s in range(1, TILES)]
 
         def sums_turned(s):
             for i in range(GROUP):
@@ -137,21 +150,21 @@ def tile_list_head_members_and_group_kernel(tc, xt_words, xt_scales, w_words, w_
             nc.scalar.activation(out=sums[s], in_=banks[s][:, 0, :], func=ACT.Copy, scale=-1.0 / GROUP)
 
         def means_back(s):
-            nc.tensor.transpose(banks[s][:, 1, :], sums[s], ident[:])
+            nc.tensor.transpose(means[s], sums[s], ident[:])
 
         def centre_psum(s):
             nc.vector.tensor_tensor(
                 out=d[s][:].rearrange("p (b i) -> p b i", i=GROUP),
                 in0=u[s][:].rearrange("p (b i) -> p b i", i=GROUP),
-                in1=banks[s][:, 1, :].unsqueeze(2).to_broadcast([P, J // GROUP, GROUP]),
+                in1=means[s].unsqueeze(2).to_broadcast([P, J // GROUP, GROUP]),
                 op=ALU.add,
             )
             nc.scalar.activation(out=th[s][:], in_=d[s][:], func=ACT.Tanh)
 
-        deal(nc, ws_codes, ws_raw)
-        deal(nc, ws_plane, ws_plane_raw)
         for s in range(TILES):
             gather(s)
+        ws_plane = keep.tile([P, N], U8, name="ws_plane", tag="z2", align_bytes=64)
+        deal(nc, ws_plane[:], ws_plane_raw[:])
         for s in range(TILES - 1):
             sums_turned(s)
         nc.scalar.copy(
@@ -163,17 +176,17 @@ def tile_list_head_members_and_group_kernel(tc, xt_words, xt_scales, w_words, w_
         for s in range(TILES - 1):
             means_turned(s)
             means_back(s)
+        sums_turned(TILES - 1)
+        means_turned(TILES - 1)
+        means_back(TILES - 1)
         nc.vector.quantize_mx(
             out=sx_codes[:].bitcast(FP8X4), scales=sx_plane[:], in_=sx_bf[:].rearrange("p j t -> p (j t)")
         )
-        group_sums(3)
-        centre_psum(0)
-        centre(3)
-        centre_psum(1)
-        centre_psum(2)
+        for s in range(TILES):
+            centre_psum(s)
 
         out_rows = out.rearrange("(a s c) j -> s a c j", a=RUNS, s=TILES)
-        for s in (0, 3, 1, 2):
+        for s in range(TILES):
             q_ps = psum.tile([P, J], F32, name="q_ps%d" % s, tag="product%d" % s)
             nc.tensor.matmul_mx(
                 out=q_ps[:],
@@ -185,5 +198,10 @@ def tile_list_head_members_and_group_kernel(tc, xt_words, xt_scales, w_words, w_
                 stop=True,
             )
             y = keep.tile([P, J], F32, name="y%d" % s)
-            nc.vector.scalar_tensor_tensor(out=y[:], in0=q_ps[:], scalar=0.5, in1=th[s][:], op0=ALU.mult, op1=ALU.add)
-            nc.sync.dma_start(out=out_rows[s], in_=y[:])
+            parts = 2 if s == TILES - 1 else 1
+            for part in range(parts):
+                cols = slice(part * J // parts, (part + 1) * J // parts)
+                nc.vector.scalar_tensor_tensor(
+                    out=y[:, cols], in0=q_ps[:, cols], scalar=0.5, in1=th[s][:, cols], op0=ALU.mult, op1=ALU.add
+                )
+                nc.sync.dma_start(out=out_rows[s][:, :, cols], in_=y[:, cols])

@@ -49,31 +49,36 @@ def tile_list_head_members_and_group_kernel(tc, xt_words, xt_scales, w_words, w_
         w_plane_raw = keep.tile([P, N], U8, name="w_plane_raw", align_bytes=64)
         w_codes = keep.tile([P, 2 * N], U8, name="w_codes", align_bytes=64)
         w_plane = keep.tile([P, N], U8, name="w_plane", align_bytes=64)
-        ws_plane_raw = keep.tile([P, N], U8, name="ws_plane_raw", align_bytes=64)
         ws_codes = keep.tile([P, N], U32, name="ws_codes", align_bytes=64)
-        sx_bf = keep.tile([P, J, 4], BF16, name="sx_bf", align_bytes=64)
+        sx_bf = keep.tile([P, J, 4], BF16, name="sx_bf", tag="sx_bf", align_bytes=64)
         sx_codes = keep.tile([P, J], U32, name="sx_codes", align_bytes=64)
         sx_plane = keep.tile([P, J], U8, name="sx_plane", align_bytes=64)
 
         ident = keep.tile([P, P], F32, name="ident")
-        warm_in = keep.tile([P, 8], F32, name="warm_in", tag="ws_raw", align_bytes=64)
-        warm_out = keep.tile([P, 8], F32, name="warm_out", tag="sx_raw", align_bytes=64)
+        warm = keep.tile([P, 8], F32, name="warm", tag="sx_raw0", align_bytes=64)
+        warm_out = keep.tile([P, 8], F32, name="warm_out", tag="sx_raw1", align_bytes=64)
+        ws_raw = keep.tile([P, N], U32, name="ws_raw", align_bytes=64)
+        z_sb = [keep.tile([P, 2 * T], F32, name="z%d" % s, tag="z%d" % s, align_bytes=64) for s in range(TILES)]
         nc.gpsimd.memset(xt_plane[:].bitcast(I32), 0)
-        nc.gpsimd.memset(warm_in[:], 0.0)
+        nc.gpsimd.memset(warm[:], 0.0)
         nc.vector.memset(w_plane[:].bitcast(I32), 0)
-        nc.gpsimd.memset(ws_plane_raw[:].bitcast(I32), 0)
+        for s in range(TILES):
+            nc.vector.memset(z_sb[s][:, T:], 0.0)
         make_identity(nc, ident[:])
 
         load_scale_rows([nc.sync] * 4, w_plane_raw, w_scales)
         nc.sync.dma_start(out=w_raw[:].bitcast(I32), in_=w_words[0].bitcast(I32))
-        nc.scalar.dma_start(out=xt_codes[:].bitcast(I32), in_=xt_words[0].rearrange("p c r -> p (c r)").bitcast(I32))
-        load_scale_rows([nc.sync] * 4, xt_plane, xt_scales)
-        nc.scalar.activation(out=warm_out[:], in_=warm_in[:], func=ACT.Tanh)
-        nc.sync.dma_start(offsets[:], offs)
-        ws_raw = keep.tile([P, N], U32, name="ws_raw", tag="ws_raw", align_bytes=64)
-        sx_raw = keep.tile([P, 4, J], F32, name="sx_raw", tag="sx_raw", align_bytes=64)
+        nc.sync.dma_start(out=xt_codes[:].bitcast(I32), in_=xt_words[0].rearrange("p c r -> p (c r)").bitcast(I32))
         nc.sync.dma_start(out=ws_raw[:].bitcast(I32), in_=ws_words[0].rearrange("p c r -> p (c r)").bitcast(I32))
-        nc.sync.dma_start(out=sx_raw[:], in_=sx.rearrange("(p i) j -> p i j", i=4))
+        load_scale_rows([nc.sync] * 4, xt_plane, xt_scales)
+        nc.scalar.activation(out=warm_out[:], in_=warm[:], func=ACT.Tanh)
+        nc.sync.dma_start(offsets[:], offs)
+        sx_rows = sx.rearrange("(p i) j -> p i j", i=4)
+        sx_raw = [keep.tile([P, 4, J // 2], F32, name="sx_raw%d" % h, tag="sx_raw%d" % h, align_bytes=64) for h in range(2)]
+        for h in range(2):
+            nc.sync.dma_start(out=sx_raw[h][:], in_=sx_rows[:, :, h * J // 2 : (h + 1) * J // 2])
+        ws_plane_raw = keep.tile([P, N], U8, name="ws_plane_raw", align_bytes=64)
+        nc.gpsimd.memset(ws_plane_raw[:].bitcast(I32), 0)
         load_scale_rows([nc.sync] * 4, ws_plane_raw, ws_scales)
 
         for quad in range(4):
@@ -93,7 +98,6 @@ def tile_list_head_members_and_group_kernel(tc, xt_words, xt_scales, w_words, w_
                 stop=True,
             )
 
-        z_sb = [keep.tile([P, T], F32, name="z%d" % s, tag="z%d" % s, align_bytes=64) for s in range(TILES)]
         first_half = psum.tile([P, T // 2], F32, name="first_half", tag="spare")
         z_product(0, first_half[:], slice(0, T // 2))
         nc.scalar.copy(out=z_sb[0][:, : T // 2], in_=first_half[:])
@@ -101,93 +105,86 @@ def tile_list_head_members_and_group_kernel(tc, xt_words, xt_scales, w_words, w_
             z_ps = psum.tile([P, T], F32, name="z_ps%d" % s, tag="product%d" % s)
             if s == 0:
                 z_product(s, z_ps[:, T // 2 :], slice(T // 2, T))
-                nc.vector.tensor_copy(out=z_sb[s][:, T // 2 :], in_=z_ps[:, T // 2 :])
+                nc.vector.tensor_copy(out=z_sb[s][:, T // 2 : T], in_=z_ps[:, T // 2 :])
             else:
                 z_product(s, z_ps[:], slice(0, T))
-                nc.scalar.copy(out=z_sb[s][:], in_=z_ps[:])
+                nc.scalar.copy(out=z_sb[s][:, :T], in_=z_ps[:])
 
-        u, sums, d, th = [], [], [], []
-        for s in range(TILES):
-            u.append(keep.tile([P, J], F32, name="u%d" % s))
-            d.append(keep.tile([P, J], F32, name="d%d" % s))
-            th.append(keep.tile([P, J], F32, name="th%d" % s))
+        u = [keep.tile([P, J], F32, name="u%d" % s) for s in range(TILES)]
+        sums = []
 
         def gather(s):
-            for h in range(2):
-                nc.vector.tensor_copy(
-                    out=u[s][:, 256 * h : 256 * (h + 1)],
-                    in_=z_sb[s][:].indirect(offsets[:, 16 * h : 16 * (h + 1)]),
-                )
+            nc.vector.tensor_copy(out=u[s][:], in_=z_sb[s][:].indirect(offsets[:]))
 
-        def group_sums(s):
-            nc.vector.tensor_reduce(
-                out=sums[s], in_=u[s][:].rearrange("p (b i) -> p b i", i=GROUP), axis=mybir.AxisListType.X, op=ALU.add
-            )
-
-        def centre(s):
-            nc.vector.scalar_tensor_tensor(
-                out=d[s][:].rearrange("p (b i) -> p b i", i=GROUP),
-                in0=sums[s].unsqueeze(2).to_broadcast([P, J // GROUP, GROUP]),
-                scalar=-1.0 / GROUP,
-                in1=u[s][:].rearrange("p (b i) -> p b i", i=GROUP),
-                op0=ALU.mult,
-                op1=ALU.add,
-            )
-            nc.scalar.activation(out=th[s][:], in_=d[s][:], func=ACT.Tanh)
-
-        banks = [psum.tile([P, 2, P], F32, name="mean_ps%d" % s) for s in range(TILES - 1)]
-        banks.append(banks[0])
-        first_means = psum.tile([P, P], F32, name="first_means", tag="spare")
-        means = [first_means[:]] + [banks[s][:, 1, :] for s in range(1, TILES)]
+        banks = [psum.tile([P, P], F32, name="sums_ps%d" % b, tag="sums%d" % b) for b in range(2)]
+        means_bank = ["spare", "product0", "product2", "product3"]
+        means = [psum.tile([P, P], F32, name="means_ps%d" % s, tag=means_bank[s]) for s in range(TILES)]
 
         def sums_turned(s):
             for i in range(GROUP):
                 nc.tensor.matmul(
-                    banks[s][:, 0, :], lhsT=u[s][:, i::GROUP], rhs=ident[:], is_transpose=True, start=(i == 0), stop=(i == GROUP - 1)
+                    banks[s % 2][:], lhsT=u[s][:, i::GROUP], rhs=ident[:], is_transpose=True, start=(i == 0), stop=(i == GROUP - 1)
                 )
 
         def means_turned(s):
-            nc.scalar.activation(out=sums[s], in_=banks[s][:, 0, :], func=ACT.Copy, scale=-1.0 / GROUP)
+            nc.scalar.activation(out=sums[s], in_=banks[s % 2][:], func=ACT.Copy, scale=-1.0 / GROUP)
 
         def means_back(s):
-            nc.tensor.transpose(means[s], sums[s], ident[:])
+            nc.tensor.transpose(means[s][:], sums[s], ident[:])
 
-        def centre_psum(s):
-            nc.vector.tensor_tensor(
-                out=d[s][:].rearrange("p (b i) -> p b i", i=GROUP),
-                in0=u[s][:].rearrange("p (b i) -> p b i", i=GROUP),
-                in1=means[s].unsqueeze(2).to_broadcast([P, J // GROUP, GROUP]),
-                op=ALU.add,
-            )
-            nc.scalar.activation(out=th[s][:], in_=d[s][:], func=ACT.Tanh)
+        def grouped(ap):
+            return ap.rearrange("p (b i) -> p b i", i=GROUP)
+
+        def spread(ap):
+            return ap.unsqueeze(2).to_broadcast([P, J // GROUP, GROUP])
 
         for s in range(TILES):
             gather(s)
         ws_plane = keep.tile([P, N], U8, name="ws_plane", tag="z2", align_bytes=64)
         deal(nc, ws_plane[:], ws_plane_raw[:])
-        for s in range(TILES - 1):
-            sums_turned(s)
-        nc.scalar.copy(
-            out=sx_bf[:].rearrange("p (c i) t -> p c t i", i=4),
-            in_=sx_raw[:].rearrange("p t (c i) -> p c t i", i=4),
-        )
-        stats = keep.tile([P, TILES, P], F32, name="stats", tag="sx_raw", align_bytes=64)
-        sums.extend(stats[:, s, :] for s in range(TILES))
-        for s in range(TILES - 1):
+        def cast(h):
+            nc.scalar.copy(
+                out=sx_bf[:, h * J // 2 : (h + 1) * J // 2, :].rearrange("p (c i) t -> p c t i", i=4),
+                in_=sx_raw[h][:].rearrange("p t (c i) -> p c t i", i=4),
+            )
+
+        sums_turned(0)
+        sums_turned(1)
+        cast(0)
+        stats_a = keep.tile([P, P], F32, name="stats_a", tag="sx_raw0", align_bytes=64)
+        sums.append(stats_a[:])
+        means_turned(0)
+        means_back(0)
+        sums_turned(2)
+        cast(1)
+        stats = keep.tile([P, TILES - 1, P], F32, name="stats", tag="sx_raw1", align_bytes=64)
+        th = {s: keep.tile([P, J], F32, name="th%d" % s) for s in range(1, TILES)}
+        sums.extend(stats[:, s, :] for s in range(1, TILES - 1))
+        sums.append(th[1][:, :P])
+        means_turned(1)
+        means_back(1)
+        nc.scalar.copy(out=stats[:, 0, :], in_=means[0][:])
+        sums_turned(3)
+        for s in (2, 3):
             means_turned(s)
             means_back(s)
-        sums_turned(TILES - 1)
-        means_turned(TILES - 1)
-        means_back(TILES - 1)
         nc.vector.quantize_mx(
             out=sx_codes[:].bitcast(FP8X4), scales=sx_plane[:], in_=sx_bf[:].rearrange("p j t -> p (j t)")
         )
-        for s in range(TILES):
-            centre_psum(s)
+        d = {}
+        d[0] = keep.tile([P, J], F32, name="d0", tag="sx_bf", align_bytes=64)
+        nc.gpsimd.tensor_tensor(out=grouped(d[0][:]), in0=grouped(u[0][:]), in1=spread(stats[:, 0, :]), op=ALU.add)
+        for s in range(1, TILES):
+            d[s] = keep.tile([P, J], F32, name="d%d" % s, tag="d%d" % s)
+            nc.vector.tensor_tensor(out=grouped(d[s][:]), in0=grouped(u[s][:]), in1=spread(means[s][:]), op=ALU.add)
+            nc.scalar.activation(out=th[s][:], in_=d[s][:], func=ACT.Tanh)
+        th[0] = keep.tile([P, J], F32, name="th0", tag="d3")
+        nc.scalar.activation(out=th[0][:], in_=d[0][:], func=ACT.Tanh)
 
         out_rows = out.rearrange("(a s c) j -> s a c j", a=RUNS, s=TILES)
-        for s in range(TILES):
-            q_ps = psum.tile([P, J], F32, name="q_ps%d" % s, tag="product%d" % s)
+        q_bank = {1: "sums1", 2: "product2", 3: "product3", 0: "sums1"}
+        for s in (1, 2, 3, 0):
+            q_ps = psum.tile([P, J], F32, name="q_ps%d" % s, tag=q_bank[s])
             nc.tensor.matmul_mx(
                 out=q_ps[:],
                 lhsT=ws_codes[:, P * s : P * (s + 1)].bitcast(FP8X4),
@@ -198,7 +195,7 @@ def tile_list_head_members_and_group_kernel(tc, xt_words, xt_scales, w_words, w_
                 stop=True,
             )
             y = keep.tile([P, J], F32, name="y%d" % s)
-            parts = 2 if s == TILES - 1 else 1
+            parts = 2 if s == 0 else 1
             for part in range(parts):
                 cols = slice(part * J // parts, (part + 1) * J // parts)
                 nc.vector.scalar_tensor_tensor(

from contextlib import ExitStack

import concourse.mybir as mybir
from concourse.masks import make_identity

K, T, J, L, N = 512, 512, 512, 512, 512
FLOPS = 2 * K * N * T + 2 * L * N * J

F32 = mybir.dt.float32
BF16 = mybir.dt.bfloat16
I32 = mybir.dt.int32
U32 = mybir.dt.uint32
U16 = mybir.dt.uint16
U8 = mybir.dt.uint8
FP8X4 = mybir.dt.float8_e4m3fn_x4
FP4X4 = mybir.dt.float4_e2m1fn_x4
ALU = mybir.AluOpType
ACT = mybir.ActivationFunctionType

P = 128
TILES = 4
RUNS = 16
GROUP = 4


def load_scale_rows(engines, plane, scales):
    rows = scales[0].bitcast(I32)
    for quad in range(4):
        engines[quad].dma_start(out=plane[32 * quad : 32 * quad + 4, :].bitcast(I32), in_=rows[4 * quad : 4 * quad + 4, :])


def deal(nc, dst, src):
    nc.vector.tensor_copy(
        out=dst.bitcast(I32).rearrange("p (s a c) -> p s a c", s=TILES, a=RUNS),
        in_=src.bitcast(I32).rearrange("p (a s c) -> p s a c", s=TILES, a=RUNS),
    )


def tile_list_head_members_and_group_kernel(tc, xt_words, xt_scales, w_words, w_scales, sx, ws_words, ws_scales, offs, out):
    nc = tc.nc
    with ExitStack() as ctx:
        keep = ctx.enter_context(tc.tile_pool(name="keep", bufs=1))
        psum = ctx.enter_context(tc.psum_pool(name="psum", bufs=1))

        offsets = keep.tile([P, J // 16], U16, name="offsets")
        xt_codes = keep.tile([P, T], U32, name="xt_codes", align_bytes=64)
        xt_plane = keep.tile([P, T], U8, name="xt_plane", align_bytes=64)
        w_raw = keep.tile([P, 2 * N], U8, name="w_raw", align_bytes=64)
        w_plane_raw = keep.tile([P, N], U8, name="w_plane_raw", align_bytes=64)
        w_codes = keep.tile([P, 2 * N], U8, name="w_codes", align_bytes=64)
        w_plane = keep.tile([P, N], U8, name="w_plane", align_bytes=64)
        ws_codes = keep.tile([P, N], U32, name="ws_codes", align_bytes=64)
        sx_bf = keep.tile([P, J, 4], BF16, name="sx_bf", tag="sx_bf", align_bytes=64)
        sx_codes = keep.tile([P, J], U32, name="sx_codes", align_bytes=64)
        sx_plane = keep.tile([P, J], U8, name="sx_plane", align_bytes=64)

        ident = keep.tile([P, P], F32, name="ident")
        warm = keep.tile([P, 8], F32, name="warm", tag="sx_raw0", align_bytes=64)
        warm_out = keep.tile([P, 8], F32, name="warm_out", tag="sx_raw1", align_bytes=64)
        ws_raw = keep.tile([P, N], U32, name="ws_raw", align_bytes=64)
        z_sb = [keep.tile([P, 2 * T], F32, name="z%d" % s, tag="z%d" % s, align_bytes=64) for s in range(TILES)]
        nc.gpsimd.memset(xt_plane[:].bitcast(I32), 0)
        nc.gpsimd.memset(warm[:], 0.0)
        nc.vector.memset(w_plane[:].bitcast(I32), 0)
        for s in range(TILES):
            nc.vector.memset(z_sb[s][:, T:], 0.0)
        make_identity(nc, ident[:])

        load_scale_rows([nc.sync] * 4, w_plane_raw, w_scales)
        nc.sync.dma_start(out=w_raw[:].bitcast(I32), in_=w_words[0].bitcast(I32))
        nc.sync.dma_start(out=xt_codes[:].bitcast(I32), in_=xt_words[0].rearrange("p c r -> p (c r)").bitcast(I32))
        nc.sync.dma_start(out=ws_raw[:].bitcast(I32), in_=ws_words[0].rearrange("p c r -> p (c r)").bitcast(I32))
        load_scale_rows([nc.sync] * 4, xt_plane, xt_scales)
        nc.scalar.activation(out=warm_out[:], in_=warm[:], func=ACT.Tanh)
        nc.sync.dma_start(offsets[:], offs)
        sx_rows = sx.rearrange("(p i) j -> p i j", i=4)
        sx_raw = [keep.tile([P, 4, J // 2], F32, name="sx_raw%d" % h, tag="sx_raw%d" % h, align_bytes=64) for h in range(2)]
        for h in range(2):
            nc.sync.dma_start(out=sx_raw[h][:], in_=sx_rows[:, :, h * J // 2 : (h + 1) * J // 2])
        ws_plane_raw = keep.tile([P, N], U8, name="ws_plane_raw", align_bytes=64)
        nc.gpsimd.memset(ws_plane_raw[:].bitcast(I32), 0)
        load_scale_rows([nc.sync] * 4, ws_plane_raw, ws_scales)

        for quad in range(4):
            rows = slice(32 * quad, 32 * quad + 4)
            deal(nc, w_plane[rows, :], w_plane_raw[rows, :])
        deal(nc, w_codes[:], w_raw[:])
        deal(nc, ws_codes[:], ws_raw[:])

        def z_product(s, z_ps, cols):
            nc.tensor.matmul_mx(
                out=z_ps,
                lhsT=w_codes[:, 2 * P * s : 2 * P * (s + 1)].bitcast(FP4X4),
                lhsT_scale=w_plane[:, P * s : P * (s + 1)],
                rhs=xt_codes[:, cols].bitcast(FP8X4),
                rhs_scale=xt_plane[:, cols],
                start=True,
                stop=True,
            )

        first_half = psum.tile([P, T // 2], F32, name="first_half", tag="spare")
        z_product(0, first_half[:], slice(0, T // 2))
        nc.scalar.copy(out=z_sb[0][:, : T // 2], in_=first_half[:])
        for s in range(TILES):
            z_ps = psum.tile([P, T], F32, name="z_ps%d" % s, tag="product%d" % s)
            if s == 0:
                z_product(s, z_ps[:, T // 2 :], slice(T // 2, T))
                nc.vector.tensor_copy(out=z_sb[s][:, T // 2 : T], in_=z_ps[:, T // 2 :])
            else:
                z_product(s, z_ps[:], slice(0, T))
                nc.scalar.copy(out=z_sb[s][:, :T], in_=z_ps[:])

        u = [keep.tile([P, J], F32, name="u%d" % s) for s in range(TILES)]
        sums = []

        def gather(s):
            nc.vector.tensor_copy(out=u[s][:], in_=z_sb[s][:].indirect(offsets[:]))

        banks = [psum.tile([P, P], F32, name="sums_ps%d" % b, tag="sums%d" % b) for b in range(2)]
        means_bank = ["spare", "product0", "product2", "product3"]
        means = [psum.tile([P, P], F32, name="means_ps%d" % s, tag=means_bank[s]) for s in range(TILES)]

        def sums_turned(s):
            for i in range(GROUP):
                nc.tensor.matmul(
                    banks[s % 2][:], lhsT=u[s][:, i::GROUP], rhs=ident[:], is_transpose=True, start=(i == 0), stop=(i == GROUP - 1)
                )

        def means_turned(s):
            nc.scalar.activation(out=sums[s], in_=banks[s % 2][:], func=ACT.Copy, scale=-1.0 / GROUP)

        def means_back(s):
            nc.tensor.transpose(means[s][:], sums[s], ident[:])

        def grouped(ap):
            return ap.rearrange("p (b i) -> p b i", i=GROUP)

        def spread(ap):
            return ap.unsqueeze(2).to_broadcast([P, J // GROUP, GROUP])

        for s in range(TILES):
            gather(s)
        ws_plane = keep.tile([P, N], U8, name="ws_plane", tag="z2", align_bytes=64)
        deal(nc, ws_plane[:], ws_plane_raw[:])
        def cast(h):
            nc.scalar.copy(
                out=sx_bf[:, h * J // 2 : (h + 1) * J // 2, :].rearrange("p (c i) t -> p c t i", i=4),
                in_=sx_raw[h][:].rearrange("p t (c i) -> p c t i", i=4),
            )

        sums_turned(0)
        sums_turned(1)
        cast(0)
        stats_a = keep.tile([P, P], F32, name="stats_a", tag="sx_raw0", align_bytes=64)
        sums.append(stats_a[:])
        means_turned(0)
        means_back(0)
        sums_turned(2)
        cast(1)
        stats = keep.tile([P, TILES - 1, P], F32, name="stats", tag="sx_raw1", align_bytes=64)
        th = {s: keep.tile([P, J], F32, name="th%d" % s) for s in range(1, TILES)}
        sums.extend(stats[:, s, :] for s in range(1, TILES - 1))
        sums.append(th[1][:, :P])
        means_turned(1)
        means_back(1)
        nc.scalar.copy(out=stats[:, 0, :], in_=means[0][:])
        sums_turned(3)
        for s in (2, 3):
            means_turned(s)
            means_back(s)
        nc.vector.quantize_mx(
            out=sx_codes[:].bitcast(FP8X4), scales=sx_plane[:], in_=sx_bf[:].rearrange("p j t -> p (j t)")
        )
        d = {}
        d[0] = keep.tile([P, J], F32, name="d0", tag="sx_bf", align_bytes=64)
        nc.gpsimd.tensor_tensor(out=grouped(d[0][:]), in0=grouped(u[0][:]), in1=spread(stats[:, 0, :]), op=ALU.add)
        for s in range(1, TILES):
            d[s] = keep.tile([P, J], F32, name="d%d" % s, tag="d%d" % s)
            nc.vector.tensor_tensor(out=grouped(d[s][:]), in0=grouped(u[s][:]), in1=spread(means[s][:]), op=ALU.add)
            nc.scalar.activation(out=th[s][:], in_=d[s][:], func=ACT.Tanh)
        th[0] = keep.tile([P, J], F32, name="th0", tag="d3")
        nc.scalar.activation(out=th[0][:], in_=d[0][:], func=ACT.Tanh)

        out_rows = out.rearrange("(a s c) j -> s a c j", a=RUNS, s=TILES)
        q_bank = {1: "sums1", 2: "product2", 3: "product3", 0: "sums1"}
        for s in (1, 2, 3, 0):
            q_ps = psum.tile([P, J], F32, name="q_ps%d" % s, tag=q_bank[s])
            nc.tensor.matmul_mx(
                out=q_ps[:],
                lhsT=ws_codes[:, P * s : P * (s + 1)].bitcast(FP8X4),
                lhsT_scale=ws_plane[:, P * s : P * (s + 1)],
                rhs=sx_codes[:].bitcast(FP8X4),
                rhs_scale=sx_plane[:],
                start=True,
                stop=True,
            )
            y = keep.tile([P, J], F32, name="y%d" % s)
            parts = 2 if s == 0 else 1
            for part in range(parts):
                cols = slice(part * J // parts, (part + 1) * J // parts)
                nc.vector.scalar_tensor_tensor(
                    out=y[:, cols], in0=q_ps[:, cols], scalar=0.5, in1=th[s][:, cols], op0=ALU.mult, op1=ALU.add
                )
                nc.sync.dma_start(out=out_rows[s][:, :, cols], in_=y[:, cols])
